import numpy as np, ml_dtypes
CORES = [12,28,60,100,156,228]
N = 6
import mx_ref
NC = 128
BF = ml_dtypes.bfloat16
def setup_inputs(rng):
    def f(*shape):
        return mx_ref.flush((rng.standard_normal(shape, dtype=np.float32) * np.exp2(rng.integers(-2, 3, shape[:-1] + (1,)))).astype(BF))
    return {"w": f(N, 128, 512), "x": f(N, 128, N * 4 * NC)}
def setup_inputs_blocks(rng):
    d = setup_inputs(rng)
    for k in ("w", "x"): d[k] = mx_ref.spread(d[k], rng, 4)
    return d
def setup_inputs_wide(rng):
    d = setup_inputs(rng)
    for k in ("w", "x"): d[k] = mx_ref.flush((d[k].astype(np.float32) * np.exp2(rng.integers(-8, 9, (N, 1, 1))).astype(np.float32)).astype(BF))
    return d
def setup_inputs_zeros(rng):
    d = setup_inputs(rng); v = d["x"].reshape(N, 128, -1, 4).copy()
    v[np.broadcast_to((rng.random((N, 1, v.shape[2], 1)) < 0.33), v.shape)] = 0
    d["x"] = v.reshape(d["x"].shape)
    return d
def reference(w, x):
    y = np.zeros((N, 128, N * NC), np.float32)
    for r in range(N):
        qw = mx_ref.quantize(w[r])
        for j in range(N):
            y[r][:, NC * j:NC * j + NC] = mx_ref.matmul(qw, mx_ref.quantize(x[j][:, 4 * NC * r:4 * NC * r + 4 * NC]))
    return {"y": y}

@@ -1,0 +1,202 @@
+from concourse.bass import DstId, RemoteDMATransfer
+from concourse.mybir import dt, ActivationFunctionType
+
+N = 6
+TC = 128
+TB = 4 * TC
+BANK = 512
+
+SCRATCH = {
+    "xb": ("sbuf", [128, N * TB], "bfloat16"),
+    "wb": ("sbuf", [128, TB], "bfloat16"),
+    "wq": ("sbuf", [128, TC], "float8_e4m3fn_x4"),
+    "ws": ("sbuf", [128, TC], "uint8"),
+    "xq": ("sbuf", [128, (N - 1) * TC], "float8_e4m3fn_x4"),
+    "xs": ("sbuf", [128, (N - 1) * TC], "uint8"),
+    "rq": ("sbuf", [128, N * TC], "float8_e4m3fn_x4"),
+    "rs": ("sbuf", [128, N * TC], "uint8"),
+    "ps": ("psum", [128, N * BANK], "float32"),
+    "yb": ("sbuf", [128, N * TC], "float32"),
+}
+SEMAPHORES = (["ld%d" % r for r in range(N)] + ["ldw"] + ["q%d" % r for r in range(N)] + ["qw"]
+              + ["arr%d" % j for j in range(N)] + ["mm%d" % j for j in range(N)] + ["cp%d" % j for j in range(N)]
+              + ["st_a", "st_b", "sent", "hin"])
+
+
+def _bits(mask):
+    return [b for b in range(mask.bit_length()) if (mask >> b) & 1]
+
+
+def _pick(mask, part, parts):
+    b = _bits(mask)
+    n = len(b) // parts
+    return sum(1 << e for e in b[part * n:(part + 1) * n])
+
+
+def _count(mask):
+    return len(_bits(mask))
+
+
+def _plan(cores, topo):
+    n = len(cores)
+    plans = []
+    for j, cj in enumerate(cores):
+        near = [r for r in range(n) if r != j and topo.may_write(cj, cores[r])]
+        far = [r for r in range(n) if r != j and not topo.may_write(cj, cores[r])]
+        club = sorted(near + [j])
+        k = club.index(j)
+        direct = club[k ^ 1]
+        via = far + [r for r in near if r != direct]
+        odd = k % 2
+        if len(far) == len(via):
+            via = via[2 * odd:] + via[:2 * odd]
+            home_first = False
+        else:
+            home_first = (odd == 0)
+        span = topo.CORES_PER_CHIP
+        chipmates = [c for c in range(max(0, cj - span), cj + span + 1)
+                     if c != cj and topo.host(c) == topo.host(cj) and topo.chip(c) == topo.chip(cj)]
+        used, relays = [], []
+        for p in range(2):
+            home = home_first if p == 0 else not home_first
+            ok = [h for h in chipmates if h not in used and (topo.die(h) == topo.die(cj)) == home
+                  and all(topo.may_write(h, cores[r]) for r in via[2 * p:2 * p + 2])]
+            relays.append((ok[0], ok[1]))
+            used += ok[:2]
+        plans.append({"via": via, "direct": direct, "relays": relays})
+    return plans
+
+
+def _relay(g, core, T, topo, cores, j, dests, codes):
+    g.wait_ge(T.sem.hin, _feed_count(topo, cores[j], core, codes))
+    transfers, total = [], 0
+    for i, r in enumerate(dests):
+        d = cores[r]
+        rid, pid = topo.addr(d, core)
+        m = _pick(topo.mask(core, d), i, len(dests))
+        if codes:
+            src = T.rq[:, TC * i:TC * (i + 1)].bitcast(dt.uint8)
+            dst = T.rq[:, TC * j:TC * (j + 1)].bitcast(dt.uint8)
+        else:
+            src = T.rs[:, TC * i:TC * (i + 1)]
+            dst = T.rs[:, TC * j:TC * (j + 1)]
+        transfers.append(RemoteDMATransfer(dst_ids=[DstId(rid=rid, pnc=pid)], dma_engine_mask=m,
+                                           remote_sem=T.sem["arr%d" % j], src=src, dst=dst))
+        total += _count(m)
+    g.remote_dma_fused(transfers, local_sem=T.sem.sent)
+    g.wait_ge(T.sem.sent, total)
+
+
+def _feed_mask(topo, src, relay, codes, p):
+    m = topo.mask(src, relay)
+    return m if codes else _pick(m, p, 2)
+
+
+def _feed_count(topo, src, relay, codes):
+    return _count(_feed_mask(topo, src, relay, codes, 0))
+
+
+def rank_program(g, core, T, topo):
+    cores = [int(c) for c in T.cores]
+    plans = _plan(cores, topo)
+    rank = T.rank_of(core)
+    if rank is None:
+        for j, pj in enumerate(plans):
+            for p, (hc, hs) in enumerate(pj["relays"]):
+                if core in (hc, hs):
+                    _relay(g, core, T, topo, cores, j, pj["via"][2 * p:2 * p + 2], core == hc)
+        return
+
+    me = plans[rank]
+    ship = me["via"] + [me["direct"]]
+
+    queues = [g.sync, g.scalar]
+    seq = ship + ["w", rank]
+    for i, r in enumerate(seq):
+        if r == "w":
+            queues[i % 2].dma_start(T.wb[:], T.w[:]).then_inc(T.sem.ldw, 16)
+        else:
+            queues[i % 2].dma_start(T.xb[:, TB * r:TB * (r + 1)], T.x[:, TB * r:TB * (r + 1)]).then_inc(T.sem["ld%d" % r], 16)
+
+    for s, r in enumerate(seq):
+        if r == "w":
+            g.vector.wait_ge(T.sem.ldw, 16)
+            g.vector.quantize_mx(T.wq[:], T.ws[:], T.wb[:]).then_inc(T.sem.qw, 1)
+            continue
+        g.vector.wait_ge(T.sem["ld%d" % r], 16)
+        if r == rank:
+            oq, os_ = T.rq[:, TC * r:TC * (r + 1)], T.rs[:, TC * r:TC * (r + 1)]
+        else:
+            oq, os_ = T.xq[:, TC * s:TC * (s + 1)], T.xs[:, TC * s:TC * (s + 1)]
+        g.vector.quantize_mx(oq, os_, T.xb[:, TB * r:TB * (r + 1)]).then_inc(T.sem["q%d" % r], 1)
+
+    sent = 0
+    for p in range(2):
+        for r in ship[2 * p:2 * p + 2]:
+            g.wait_ge(T.sem["q%d" % r], 1)
+        hc = me["relays"][p][0]
+        rid, pid = topo.addr(hc, core)
+        m = _feed_mask(topo, core, hc, True, p)
+        g.remote_dma(out_ap=T.rq[:, 0:2 * TC].bitcast(dt.uint8),
+                     in_ap=T.xq[:, 2 * TC * p:2 * TC * (p + 1)].bitcast(dt.uint8),
+                     remote_sem=T.sem.hin, local_sem=T.sem.sent, pid=pid, routing_id=rid, dma_engine_mask=m)
+        sent += _count(m)
+    planes = []
+    for p in range(2):
+        hs = me["relays"][p][1]
+        rid, pid = topo.addr(hs, core)
+        m = _feed_mask(topo, core, hs, False, p)
+        planes.append(RemoteDMATransfer(dst_ids=[DstId(rid=rid, pnc=pid)], dma_engine_mask=m, remote_sem=T.sem.hin,
+                                        src=T.xs[:, 2 * TC * p:2 * TC * (p + 1)], dst=T.rs[:, 0:2 * TC]))
+        sent += _count(m)
+    g.remote_dma_fused(planes, local_sem=T.sem.sent)
+    d = cores[me["direct"]]
+    rid, pid = topo.addr(d, core)
+    m = topo.mask(core, d)
+    g.wait_ge(T.sem["q%d" % me["direct"]], 1)
+    g.remote_dma(out_ap=T.rq[:, TC * rank:TC * (rank + 1)].bitcast(dt.uint8),
+                 in_ap=T.xq[:, 4 * TC:5 * TC].bitcast(dt.uint8),
+                 remote_sem=T.sem["arr%d" % rank], local_sem=T.sem.sent, pid=pid, routing_id=rid, dma_engine_mask=m)
+    g.remote_dma(out_ap=T.rs[:, TC * rank:TC * (rank + 1)], in_ap=T.xs[:, 4 * TC:5 * TC],
+                 remote_sem=T.sem["arr%d" % rank], local_sem=T.sem.sent, pid=pid, routing_id=rid, dma_engine_mask=m)
+    sent += 2 * _count(m)
+    g.wait_ge(T.sem.sent, sent)
+
+    def stage(j):
+        if j == rank:
+            return 0
+        if plans[j]["direct"] == rank:
+            return 1
+        return 2 + plans[j]["via"].index(rank) // 2
+
+    def need(j):
+        if plans[j]["direct"] == rank:
+            return 2 * _count(topo.mask(cores[j], core))
+        p = plans[j]["via"].index(rank) // 2
+        return sum(_count(_pick(topo.mask(h, core), 0, 2)) for h in plans[j]["relays"][p])
+
+    proc = sorted(range(N), key=lambda j: (stage(j), j))
+    g.tensor.wait_ge(T.sem.qw, 1)
+    stores = [0, 0]
+    for k, j in enumerate(proc):
+        if j == rank:
+            g.tensor.wait_ge(T.sem["q%d" % j], 1)
+        else:
+            g.tensor.wait_ge(T.sem["arr%d" % j], need(j))
+        bank = T.ps[:, BANK * k:BANK * k + TC]
+        g.tensor.matmul_mx(bank, T.wq[:], T.ws[:], T.rq[:, TC * j:TC * (j + 1)], T.rs[:, TC * j:TC * (j + 1)],
+                           True, True).then_inc(T.sem["mm%d" % j], 1)
+        blk = T.yb[:, TC * j:TC * (j + 1)]
+        if k % 2 == 0:
+            g.vector.wait_ge(T.sem["mm%d" % j], 1)
+            g.vector.tensor_copy(blk, bank).then_inc(T.sem["cp%d" % j], 1)
+            q, st = g.sync, T.sem.st_a
+        else:
+            g.scalar.wait_ge(T.sem["mm%d" % j], 1)
+            g.scalar.activation(blk, bank, ActivationFunctionType.Copy).then_inc(T.sem["cp%d" % j], 1)
+            q, st = g.scalar, T.sem.st_b
+        q.wait_ge(T.sem["cp%d" % j], 1)
+        q.dma_start(T.y[:, TC * j:TC * (j + 1)], blk).then_inc(st, 16)
+        stores[k % 2] += 16
+    g.sync.wait_ge(T.sem.st_a, stores[0])
+    g.scalar.wait_ge(T.sem.st_b, stores[1])

@@ -2,6 +2,7 @@ from concourse.bass import DstId, RemoteDMATransfer
 from concourse.mybir import dt, ActivationFunctionType
 
 N = 6
+NR = 4
 TC = 128
 TB = 4 * TC
 BANK = 512
@@ -20,7 +21,7 @@ SCRATCH = {
 }
 SEMAPHORES = (["ld%d" % r for r in range(N)] + ["ldw"] + ["q%d" % r for r in range(N)] + ["qw"]
               + ["arr%d" % j for j in range(N)] + ["mm%d" % j for j in range(N)] + ["cp%d" % j for j in range(N)]
-              + ["st_a", "st_b", "sent", "hin"])
+              + ["st_a", "st_b", "sent", "hin_s", "hin_c"])
 
 
 def _bits(mask):
@@ -56,44 +57,32 @@ def _plan(cores, topo):
         span = topo.CORES_PER_CHIP
         chipmates = [c for c in range(max(0, cj - span), cj + span + 1)
                      if c != cj and topo.host(c) == topo.host(cj) and topo.chip(c) == topo.chip(cj)]
-        used, relays = [], []
+        relays = []
         for p in range(2):
             home = home_first if p == 0 else not home_first
-            ok = [h for h in chipmates if h not in used and (topo.die(h) == topo.die(cj)) == home
+            ok = [h for h in chipmates if h not in relays and (topo.die(h) == topo.die(cj)) == home
                   and all(topo.may_write(h, cores[r]) for r in via[2 * p:2 * p + 2])]
-            relays.append((ok[0], ok[1]))
-            used += ok[:2]
+            relays += ok[:2]
         plans.append({"via": via, "direct": direct, "relays": relays})
     return plans
 
 
-def _relay(g, core, T, topo, cores, j, dests, codes):
-    g.wait_ge(T.sem.hin, _feed_count(topo, cores[j], core, codes))
-    transfers, total = [], 0
-    for i, r in enumerate(dests):
-        d = cores[r]
-        rid, pid = topo.addr(d, core)
-        m = _pick(topo.mask(core, d), i, len(dests))
-        if codes:
-            src = T.rq[:, TC * i:TC * (i + 1)].bitcast(dt.uint8)
-            dst = T.rq[:, TC * j:TC * (j + 1)].bitcast(dt.uint8)
-        else:
-            src = T.rs[:, TC * i:TC * (i + 1)]
-            dst = T.rs[:, TC * j:TC * (j + 1)]
-        transfers.append(RemoteDMATransfer(dst_ids=[DstId(rid=rid, pnc=pid)], dma_engine_mask=m,
-                                           remote_sem=T.sem["arr%d" % j], src=src, dst=dst))
-        total += _count(m)
-    g.remote_dma_fused(transfers, local_sem=T.sem.sent)
-    g.wait_ge(T.sem.sent, total)
+def _feed_mask(topo, src, relay, k):
+    return _pick(topo.mask(src, relay), k, NR)
 
 
-def _feed_mask(topo, src, relay, codes, p):
-    m = topo.mask(src, relay)
-    return m if codes else _pick(m, p, 2)
-
-
-def _feed_count(topo, src, relay, codes):
-    return _count(_feed_mask(topo, src, relay, codes, 0))
+def _relay(g, core, T, topo, cores, j, k, r):
+    fed = _count(_feed_mask(topo, cores[j], core, k))
+    d = cores[r]
+    rid, pid = topo.addr(d, core)
+    m = topo.mask(core, d)
+    g.wait_ge(T.sem.hin_s, fed)
+    g.remote_dma(out_ap=T.rs[:, TC * j:TC * (j + 1)], in_ap=T.rs[:, 0:TC],
+                 remote_sem=T.sem["arr%d" % j], local_sem=T.sem.sent, pid=pid, routing_id=rid, dma_engine_mask=m)
+    g.wait_ge(T.sem.hin_c, fed)
+    g.remote_dma(out_ap=T.rq[:, TC * j:TC * (j + 1)].bitcast(dt.uint8), in_ap=T.rq[:, 0:TC].bitcast(dt.uint8),
+                 remote_sem=T.sem["arr%d" % j], local_sem=T.sem.sent, pid=pid, routing_id=rid, dma_engine_mask=m)
+    g.wait_ge(T.sem.sent, 2 * _count(m))
 
 
 def rank_program(g, core, T, topo):
@@ -102,9 +91,9 @@ def rank_program(g, core, T, topo):
     rank = T.rank_of(core)
     if rank is None:
         for j, pj in enumerate(plans):
-            for p, (hc, hs) in enumerate(pj["relays"]):
-                if core in (hc, hs):
-                    _relay(g, core, T, topo, cores, j, pj["via"][2 * p:2 * p + 2], core == hc)
+            if core in pj["relays"]:
+                k = pj["relays"].index(core)
+                _relay(g, core, T, topo, cores, j, k, pj["via"][k])
         return
 
     me = plans[rank]
@@ -130,50 +119,49 @@ def rank_program(g, core, T, topo):
             oq, os_ = T.xq[:, TC * s:TC * (s + 1)], T.xs[:, TC * s:TC * (s + 1)]
         g.vector.quantize_mx(oq, os_, T.xb[:, TB * r:TB * (r + 1)]).then_inc(T.sem["q%d" % r], 1)
 
-    sent = 0
-    for p in range(2):
-        for r in ship[2 * p:2 * p + 2]:
-            g.wait_ge(T.sem["q%d" % r], 1)
-        hc = me["relays"][p][0]
-        rid, pid = topo.addr(hc, core)
-        m = _feed_mask(topo, core, hc, True, p)
-        g.remote_dma(out_ap=T.rq[:, 0:2 * TC].bitcast(dt.uint8),
-                     in_ap=T.xq[:, 2 * TC * p:2 * TC * (p + 1)].bitcast(dt.uint8),
-                     remote_sem=T.sem.hin, local_sem=T.sem.sent, pid=pid, routing_id=rid, dma_engine_mask=m)
-        sent += _count(m)
-    planes = []
-    for p in range(2):
-        hs = me["relays"][p][1]
-        rid, pid = topo.addr(hs, core)
-        m = _feed_mask(topo, core, hs, False, p)
-        planes.append(RemoteDMATransfer(dst_ids=[DstId(rid=rid, pnc=pid)], dma_engine_mask=m, remote_sem=T.sem.hin,
-                                        src=T.xs[:, 2 * TC * p:2 * TC * (p + 1)], dst=T.rs[:, 0:2 * TC]))
-        sent += _count(m)
-    g.remote_dma_fused(planes, local_sem=T.sem.sent)
+    sent = [0]
+
+    def feed(k, codes):
+        h = me["relays"][k]
+        rid, pid = topo.addr(h, core)
+        m = _feed_mask(topo, core, h, k)
+        sent[0] += _count(m)
+        if codes:
+            return RemoteDMATransfer(dst_ids=[DstId(rid=rid, pnc=pid)], dma_engine_mask=m, remote_sem=T.sem.hin_c,
+                                     src=T.xq[:, TC * k:TC * (k + 1)].bitcast(dt.uint8),
+                                     dst=T.rq[:, 0:TC].bitcast(dt.uint8))
+        return RemoteDMATransfer(dst_ids=[DstId(rid=rid, pnc=pid)], dma_engine_mask=m, remote_sem=T.sem.hin_s,
+                                 src=T.xs[:, TC * k:TC * (k + 1)], dst=T.rs[:, 0:TC])
+
+    g.wait_ge(T.sem["q%d" % ship[0]], 1)
+    g.remote_dma_fused([feed(0, False)], local_sem=T.sem.sent)
+    for r in ship[1:NR]:
+        g.wait_ge(T.sem["q%d" % r], 1)
+    g.remote_dma_fused([feed(k, False) for k in range(1, NR)], local_sem=T.sem.sent)
+    g.remote_dma_fused([feed(k, True) for k in range(NR)], local_sem=T.sem.sent)
     d = cores[me["direct"]]
     rid, pid = topo.addr(d, core)
     m = topo.mask(core, d)
     g.wait_ge(T.sem["q%d" % me["direct"]], 1)
     g.remote_dma(out_ap=T.rq[:, TC * rank:TC * (rank + 1)].bitcast(dt.uint8),
-                 in_ap=T.xq[:, 4 * TC:5 * TC].bitcast(dt.uint8),
+                 in_ap=T.xq[:, NR * TC:(NR + 1) * TC].bitcast(dt.uint8),
                  remote_sem=T.sem["arr%d" % rank], local_sem=T.sem.sent, pid=pid, routing_id=rid, dma_engine_mask=m)
-    g.remote_dma(out_ap=T.rs[:, TC * rank:TC * (rank + 1)], in_ap=T.xs[:, 4 * TC:5 * TC],
+    g.remote_dma(out_ap=T.rs[:, TC * rank:TC * (rank + 1)], in_ap=T.xs[:, NR * TC:(NR + 1) * TC],
                  remote_sem=T.sem["arr%d" % rank], local_sem=T.sem.sent, pid=pid, routing_id=rid, dma_engine_mask=m)
-    sent += 2 * _count(m)
-    g.wait_ge(T.sem.sent, sent)
+    sent[0] += 2 * _count(m)
+    g.wait_ge(T.sem.sent, sent[0])
 
     def stage(j):
         if j == rank:
             return 0
         if plans[j]["direct"] == rank:
             return 1
-        return 2 + plans[j]["via"].index(rank) // 2
+        return 2 + plans[j]["via"].index(rank)
 
     def need(j):
         if plans[j]["direct"] == rank:
             return 2 * _count(topo.mask(cores[j], core))
-        p = plans[j]["via"].index(rank) // 2
-        return sum(_count(_pick(topo.mask(h, core), 0, 2)) for h in plans[j]["relays"][p])
+        return 2 * _count(topo.mask(plans[j]["relays"][plans[j]["via"].index(rank)], core))
 
     proc = sorted(range(N), key=lambda j: (stage(j), j))
     g.tensor.wait_ge(T.sem.qw, 1)

from concourse.bass import DstId, RemoteDMATransfer
from concourse.mybir import dt, ActivationFunctionType

N = 6
NR = 4
TC = 128
TB = 4 * TC
BANK = 512

SCRATCH = {
    "xb": ("sbuf", [128, N * TB], "bfloat16"),
    "wb": ("sbuf", [128, TB], "bfloat16"),
    "wq": ("sbuf", [128, TC], "float8_e4m3fn_x4"),
    "ws": ("sbuf", [128, TC], "uint8"),
    "xq": ("sbuf", [128, (N - 1) * TC], "float8_e4m3fn_x4"),
    "xs": ("sbuf", [128, (N - 1) * TC], "uint8"),
    "rq": ("sbuf", [128, N * TC], "float8_e4m3fn_x4"),
    "rs": ("sbuf", [128, N * TC], "uint8"),
    "ps": ("psum", [128, N * BANK], "float32"),
    "yb": ("sbuf", [128, N * TC], "float32"),
}
SEMAPHORES = (["ld%d" % r for r in range(N)] + ["ldw"] + ["q%d" % r for r in range(N)] + ["qw"]
              + ["arr%d" % j for j in range(N)] + ["mm%d" % j for j in range(N)] + ["cp%d" % j for j in range(N)]
              + ["st_a", "st_b", "sent", "hin_s", "hin_c"])


def _bits(mask):
    return [b for b in range(mask.bit_length()) if (mask >> b) & 1]


def _pick(mask, part, parts):
    b = _bits(mask)
    n = len(b) // parts
    return sum(1 << e for e in b[part * n:(part + 1) * n])


def _count(mask):
    return len(_bits(mask))


def _plan(cores, topo):
    n = len(cores)
    plans = []
    for j, cj in enumerate(cores):
        near = [r for r in range(n) if r != j and topo.may_write(cj, cores[r])]
        far = [r for r in range(n) if r != j and not topo.may_write(cj, cores[r])]
        club = sorted(near + [j])
        k = club.index(j)
        direct = club[k ^ 1]
        via = far + [r for r in near if r != direct]
        odd = k % 2
        if len(far) == len(via):
            via = via[2 * odd:] + via[:2 * odd]
            home_first = False
        else:
            home_first = (odd == 0)
        span = topo.CORES_PER_CHIP
        chipmates = [c for c in range(max(0, cj - span), cj + span + 1)
                     if c != cj and topo.host(c) == topo.host(cj) and topo.chip(c) == topo.chip(cj)]
        relays = []
        for p in range(2):
            home = home_first if p == 0 else not home_first
            ok = [h for h in chipmates if h not in relays and (topo.die(h) == topo.die(cj)) == home
                  and all(topo.may_write(h, cores[r]) for r in via[2 * p:2 * p + 2])]
            relays += ok[:2]
        plans.append({"via": via, "direct": direct, "relays": relays})
    return plans


def _feed_mask(topo, src, relay, k):
    return _pick(topo.mask(src, relay), k, NR)


def _relay(g, core, T, topo, cores, j, k, r):
    fed = _count(_feed_mask(topo, cores[j], core, k))
    d = cores[r]
    rid, pid = topo.addr(d, core)
    m = topo.mask(core, d)
    g.wait_ge(T.sem.hin_s, fed)
    g.remote_dma(out_ap=T.rs[:, TC * j:TC * (j + 1)], in_ap=T.rs[:, 0:TC],
                 remote_sem=T.sem["arr%d" % j], local_sem=T.sem.sent, pid=pid, routing_id=rid, dma_engine_mask=m)
    g.wait_ge(T.sem.hin_c, fed)
    g.remote_dma(out_ap=T.rq[:, TC * j:TC * (j + 1)].bitcast(dt.uint8), in_ap=T.rq[:, 0:TC].bitcast(dt.uint8),
                 remote_sem=T.sem["arr%d" % j], local_sem=T.sem.sent, pid=pid, routing_id=rid, dma_engine_mask=m)
    g.wait_ge(T.sem.sent, 2 * _count(m))


def rank_program(g, core, T, topo):
    cores = [int(c) for c in T.cores]
    plans = _plan(cores, topo)
    rank = T.rank_of(core)
    if rank is None:
        for j, pj in enumerate(plans):
            if core in pj["relays"]:
                k = pj["relays"].index(core)
                _relay(g, core, T, topo, cores, j, k, pj["via"][k])
        return

    me = plans[rank]
    ship = me["via"] + [me["direct"]]

    queues = [g.sync, g.scalar]
    seq = ship + ["w", rank]
    for i, r in enumerate(seq):
        if r == "w":
            queues[i % 2].dma_start(T.wb[:], T.w[:]).then_inc(T.sem.ldw, 16)
        else:
            queues[i % 2].dma_start(T.xb[:, TB * r:TB * (r + 1)], T.x[:, TB * r:TB * (r + 1)]).then_inc(T.sem["ld%d" % r], 16)

    for s, r in enumerate(seq):
        if r == "w":
            g.vector.wait_ge(T.sem.ldw, 16)
            g.vector.quantize_mx(T.wq[:], T.ws[:], T.wb[:]).then_inc(T.sem.qw, 1)
            continue
        g.vector.wait_ge(T.sem["ld%d" % r], 16)
        if r == rank:
            oq, os_ = T.rq[:, TC * r:TC * (r + 1)], T.rs[:, TC * r:TC * (r + 1)]
        else:
            oq, os_ = T.xq[:, TC * s:TC * (s + 1)], T.xs[:, TC * s:TC * (s + 1)]
        g.vector.quantize_mx(oq, os_, T.xb[:, TB * r:TB * (r + 1)]).then_inc(T.sem["q%d" % r], 1)

    sent = [0]

    def feed(k, codes):
        h = me["relays"][k]
        rid, pid = topo.addr(h, core)
        m = _feed_mask(topo, core, h, k)
        sent[0] += _count(m)
        if codes:
            return RemoteDMATransfer(dst_ids=[DstId(rid=rid, pnc=pid)], dma_engine_mask=m, remote_sem=T.sem.hin_c,
                                     src=T.xq[:, TC * k:TC * (k + 1)].bitcast(dt.uint8),
                                     dst=T.rq[:, 0:TC].bitcast(dt.uint8))
        return RemoteDMATransfer(dst_ids=[DstId(rid=rid, pnc=pid)], dma_engine_mask=m, remote_sem=T.sem.hin_s,
                                 src=T.xs[:, TC * k:TC * (k + 1)], dst=T.rs[:, 0:TC])

    g.wait_ge(T.sem["q%d" % ship[0]], 1)
    g.remote_dma_fused([feed(0, False)], local_sem=T.sem.sent)
    for r in ship[1:NR]:
        g.wait_ge(T.sem["q%d" % r], 1)
    g.remote_dma_fused([feed(k, False) for k in range(1, NR)], local_sem=T.sem.sent)
    g.remote_dma_fused([feed(k, True) for k in range(NR)], local_sem=T.sem.sent)
    d = cores[me["direct"]]
    rid, pid = topo.addr(d, core)
    m = topo.mask(core, d)
    g.wait_ge(T.sem["q%d" % me["direct"]], 1)
    g.remote_dma(out_ap=T.rq[:, TC * rank:TC * (rank + 1)].bitcast(dt.uint8),
                 in_ap=T.xq[:, NR * TC:(NR + 1) * TC].bitcast(dt.uint8),
                 remote_sem=T.sem["arr%d" % rank], local_sem=T.sem.sent, pid=pid, routing_id=rid, dma_engine_mask=m)
    g.remote_dma(out_ap=T.rs[:, TC * rank:TC * (rank + 1)], in_ap=T.xs[:, NR * TC:(NR + 1) * TC],
                 remote_sem=T.sem["arr%d" % rank], local_sem=T.sem.sent, pid=pid, routing_id=rid, dma_engine_mask=m)
    sent[0] += 2 * _count(m)
    g.wait_ge(T.sem.sent, sent[0])

    def stage(j):
        if j == rank:
            return 0
        if plans[j]["direct"] == rank:
            return 1
        return 2 + plans[j]["via"].index(rank)

    def need(j):
        if plans[j]["direct"] == rank:
            return 2 * _count(topo.mask(cores[j], core))
        return 2 * _count(topo.mask(plans[j]["relays"][plans[j]["via"].index(rank)], core))

    proc = sorted(range(N), key=lambda j: (stage(j), j))
    g.tensor.wait_ge(T.sem.qw, 1)
    stores = [0, 0]
    for k, j in enumerate(proc):
        if j == rank:
            g.tensor.wait_ge(T.sem["q%d" % j], 1)
        else:
            g.tensor.wait_ge(T.sem["arr%d" % j], need(j))
        bank = T.ps[:, BANK * k:BANK * k + TC]
        g.tensor.matmul_mx(bank, T.wq[:], T.ws[:], T.rq[:, TC * j:TC * (j + 1)], T.rs[:, TC * j:TC * (j + 1)],
                           True, True).then_inc(T.sem["mm%d" % j], 1)
        blk = T.yb[:, TC * j:TC * (j + 1)]
        if k % 2 == 0:
            g.vector.wait_ge(T.sem["mm%d" % j], 1)
            g.vector.tensor_copy(blk, bank).then_inc(T.sem["cp%d" % j], 1)
            q, st = g.sync, T.sem.st_a
        else:
            g.scalar.wait_ge(T.sem["mm%d" % j], 1)
            g.scalar.activation(blk, bank, ActivationFunctionType.Copy).then_inc(T.sem["cp%d" % j], 1)
            q, st = g.scalar, T.sem.st_b
        q.wait_ge(T.sem["cp%d" % j], 1)
        q.dma_start(T.y[:, TC * j:TC * (j + 1)], blk).then_inc(st, 16)
        stores[k % 2] += 16
    g.sync.wait_ge(T.sem.st_a, stores[0])
    g.scalar.wait_ge(T.sem.st_b, stores[1])
